import numpy as np
import ml_dtypes


def mxq(x, axis, fmt="e4m3"):
    dtype, down = {"e4m3": (ml_dtypes.float8_e4m3fn, 7), "e5m2": (ml_dtypes.float8_e5m2, 14)}[fmt]
    v = np.moveaxis(np.asarray(x, np.float32).astype(ml_dtypes.bfloat16).astype(np.float64), axis, -1)
    blocks = v.reshape(v.shape[:-1] + (-1, 32))
    amax = np.abs(blocks).max(-1, keepdims=True)
    byte = np.maximum(np.where(amax > 0, np.frexp(amax)[1] - 1 + 127, 0) - down, 1)
    scale = np.exp2(byte - 127.0)
    codes = (blocks / scale).astype(np.float32).astype(dtype).astype(np.float64)
    return np.moveaxis((codes * scale).reshape(v.shape), -1, axis)


WIDE = False


def mx_kscale(k):
    if not WIDE:
        return np.ones(k)
    levels = np.array([10, -10, 5, -5, 0])
    if k % 512:
        return np.exp2(np.random.permutation(np.resize(levels, k // 32))).repeat(32)
    a = np.empty((k // 512, 16))
    for p in range(k // 512):
        a[p, :8] = np.random.permutation(np.resize(levels, 8))
        for g in range(8):
            far = levels[np.abs(levels - a[p, g]) >= 10]
            a[p, g + 8] = far[np.random.randint(len(far))]
    return np.exp2(a.ravel()).repeat(32)


def f64(x):
    return np.asarray(x).astype(np.float64)


def striped(idx):
    return np.tile(idx.reshape(-1, 16).T, (8, 1)).astype(np.uint16)


def unstriped(offs):
    return offs[:16].T.reshape(-1).astype(np.int64)


E2M1 = np.array([0.0, 0.5, 1.0, 1.5, 2.0, 3.0, 4.0, 6.0, -0.0, -0.5, -1.0, -1.5, -2.0, -3.0, -4.0, -6.0])


def pack_weight(w, fmt):
    k, n = w.shape
    w = f64(np.asarray(w, np.float32).astype(ml_dtypes.bfloat16)).reshape(k // 32, 32, n)
    amax = np.abs(w).max(1)
    if fmt == "e4m3":
        byte = np.frexp(amax)[1] - 1 + 127 - 7
    else:
        mant, ex = np.frexp(amax / 6.0)
        byte = np.where(mant > 0.5, ex, ex - 1) + 127
    byte = np.clip(np.where(amax > 0, byte, 1), 1, 254)
    scaled = (w * np.exp2(127.0 - byte)[:, None, :]).reshape(k, n).astype(np.float32)
    by_word = np.ascontiguousarray(scaled.reshape(k // 512, 128, 4, n).transpose(0, 1, 3, 2))
    if fmt == "e4m3":
        words = by_word.astype(ml_dtypes.float8_e4m3fn).view(np.uint8)
    else:
        c = by_word.astype(ml_dtypes.float4_e2m1fn).view(np.uint8) & 0xF
        words = (c[..., 0::2] | (c[..., 1::2] << 4)).reshape(k // 512, 128, 2 * n)
    return np.ascontiguousarray(words), np.ascontiguousarray(byte.astype(np.uint8).reshape(k // 512, 16, n))


def unpack_weight(words, scales, fmt):
    g, _, n = scales.shape
    words = np.ascontiguousarray(words).reshape(g, 128, n, -1)
    if fmt == "e4m3":
        vals = words.view(ml_dtypes.float8_e4m3fn).astype(np.float64)
    else:
        nib = np.empty((g, 128, n, 4), np.uint8)
        nib[..., 0::2] = words & 0xF
        nib[..., 1::2] = words >> 4
        vals = E2M1[nib]
    vals = vals * np.repeat(np.exp2(scales.astype(np.float64) - 127.0), 8, axis=1)[..., None]
    return vals.transpose(0, 1, 3, 2).reshape(g * 512, n)


K, T, E, C, N = 384, 512, 8, 256, 512
TOP = 4


def by_expert(wq, xq):
    return np.concatenate([wq[e].T @ xq[:, e * C:(e + 1) * C] for e in range(E)], axis=1)


def setup_inputs():
    n = np.random.standard_normal
    s = mx_kscale(N)[:, None]
    deal = np.repeat(np.arange(E), C).reshape(TOP, T)[:, np.random.permutation(T)]
    deal = np.take_along_axis(deal, np.argsort(np.random.rand(TOP, T), axis=0), axis=0)
    for _ in range(8):
        s_, t_ = np.random.permutation(T).reshape(2, -1); r = np.random.randint(TOP, size=T // 2); x, y = deal[r, s_].copy(), deal[r, t_].copy()
        ok = ~((deal[:, s_] == y).any(0) | (deal[:, t_] == x).any(0)); deal[r[ok], s_[ok]] = y[ok]; deal[r[ok], t_[ok]] = x[ok]
    order = np.lexsort((np.random.rand(TOP * T), deal.reshape(-1)))
    slot_token = order % T; pos = np.empty(TOP * T, np.int64); pos[order] = np.arange(TOP * T); pos = pos.reshape(TOP, T)
    g = np.random.uniform(0.5, 1.5, (TOP, T)); g = g / g.sum(0)
    w_slot = np.empty(E * C)
    for r in range(TOP): w_slot[pos[r]] = g[r]
    w = [pack_weight(m, "e2m1") for m in n((E + 1, N, K)) / np.sqrt(N) / s[None]]
    return {
        "dyT": (n((N, T)) * s).astype(np.float32),
        "w_words": np.stack([m[0] for m in w]),
        "w_scales": np.stack([m[1] for m in w]),
        "gate": np.tile(w_slot, (N, 1)).astype(np.float32),
        "offs": striped(slot_token),
        "pos1": striped(pos[0]),
        "pos2": striped(pos[1]),
        "pos3": striped(pos[2]),
        "pos4": striped(pos[3]),
    }


def reference(dyT, w_words, w_scales, gate, offs, pos1, pos2, pos3, pos4):
    idx = unstriped(offs)
    w = np.stack([unpack_weight(w_words[e], w_scales[e], "e2m1") for e in range(E + 1)])
    gq = mxq(f64(gate) * f64(dyT)[:, idx], 0, "e4m3")
    wq = w
    ds = wq[E].T @ mxq(f64(dyT), 0, "e4m3")
    dx = by_expert(wq, gq)
    return ds + dx[:, unstriped(pos1)] + dx[:, unstriped(pos2)] + dx[:, unstriped(pos3)] + dx[:, unstriped(pos4)]

@@ -1,0 +1,139 @@
+from contextlib import ExitStack
+
+import concourse.mybir as mybir
+
+K, T, E, C, N = 384, 512, 8, 256, 512
+S = E * C
+P = 128
+PACK = 4
+CH = 512
+WIN = 704
+FLOPS = 2 * K * N * (S + T)
+
+F32 = mybir.dt.float32
+BF16 = mybir.dt.bfloat16
+U32 = mybir.dt.uint32
+U16 = mybir.dt.uint16
+U8 = mybir.dt.uint8
+I32 = mybir.dt.int32
+FP8X4 = mybir.dt.float8_e4m3fn_x4
+FP4X4 = mybir.dt.float4_e2m1fn_x4
+MULT = mybir.AluOpType.mult
+ADD = mybir.AluOpType.add
+
+
+def tile_moe_bds_lin_none_kernel(tc, dyT, w_words, w_scales, gate, offs, pos1, pos2, pos3, pos4, out):
+    nc = tc.nc
+    with ExitStack() as ctx:
+        keep = ctx.enter_context(tc.tile_pool(name="keep", bufs=1))
+        ring = ctx.enter_context(tc.tile_pool(name="ring", bufs=2))
+        psum = ctx.enter_context(tc.psum_pool(name="psum", bufs=4))
+
+        offs_t = keep.tile([P, S // 16], U16, name="offs_t")
+        nc.sync.dma_start(offs_t[:], offs)
+        dy_rows = dyT.rearrange("(p j) t -> p j t", j=PACK)
+        planes = [keep.tile([P, WIN], F32, name="plane%d" % j) for j in range(PACK)]
+        gates = [keep.tile([P, CH], F32, name="gate%d" % c) for c in range(S // CH)]
+        w_sc = keep.tile([P, (E + 1) * K], U8, name="w_sc", align_bytes=64)
+        nc.gpsimd.memset(w_sc[:].bitcast(I32), 0)
+        for j in range(PACK):
+            nc.gpsimd.memset(planes[j][:, T:WIN], 0.0)
+        nc.sync.dma_start(planes[0][:, 0:T], dy_rows[:, 0, :])
+        nc.sync.dma_start(gates[0][:], gate[0:P, 0:CH])
+        for j in range(1, PACK):
+            nc.sync.dma_start(planes[j][:, 0:T], dy_rows[:, j, :])
+        sc_rows = w_scales.rearrange("e a f k -> f (e a) k").bitcast(I32)
+        w_sc_v = w_sc[:].bitcast(I32).rearrange("p (e k) -> p e k", e=E + 1)
+        for q in range(4):
+            nc.sync.dma_start(w_sc_v[32 * q : 32 * q + 4], sc_rows[4 * q : 4 * q + 4])
+        w_t = keep.tile([P, (E + 1) * 2 * K], U8, name="w_t", align_bytes=64)
+        nc.sync.dma_start(
+            w_t[:].bitcast(I32).rearrange("p (e k) -> p e k", e=E + 1),
+            w_words.rearrange("e a p k -> p (e a) k").bitcast(I32),
+        )
+        for c in range(1, S // CH):
+            nc.sync.dma_start(gates[c][:], gate[0:P, c * CH : (c + 1) * CH])
+        dy_all = keep.tile([P, PACK, T], F32, name="dy_all")
+        nc.sync.dma_start(dy_all[:], dy_rows)
+        pos_t = []
+        for r, pos in enumerate((pos1, pos2, pos3, pos4)):
+            pt = keep.tile([P, T // 16], U16, name="pos%d" % r)
+            nc.sync.dma_start(pt[:], pos)
+            pos_t.append(pt)
+
+        g_codes = keep.tile([P, S], U32, name="g_codes", align_bytes=64)
+        g_sc = [keep.tile([P, CH], U8, name="g_sc%d" % c, align_bytes=64) for c in range(S // CH)]
+        dx = [keep.tile([P, S], F32, name="dx%d" % b) for b in range(K // P)]
+        ds = [keep.tile([P, T], F32, name="ds%d" % b) for b in range(K // P)]
+
+        def weights(e, b):
+            return (
+                w_t[:, e * 2 * K + b * 2 * P : e * 2 * K + (b + 1) * 2 * P].bitcast(FP4X4),
+                w_sc[:, e * K + b * P : e * K + (b + 1) * P],
+            )
+
+        def interleave(dst, src):
+            nc.scalar.copy(
+                dst[:].rearrange("p (c i t) -> p c t i", i=4, t=PACK),
+                src[:].rearrange("p t (c i) -> p c t i", i=4),
+            )
+
+        def gather(c):
+            g4 = ring.tile([P, PACK, CH], F32, name="g4")
+            for j in range(PACK):
+                nc.vector.tensor_tensor(
+                    g4[:, j, :], planes[j][:].indirect(offs_t[:, c * CH // 16 : (c + 1) * CH // 16]), gates[c][:], MULT
+                )
+            gb = ring.tile([P, CH * PACK], BF16, name="gb", align_bytes=64)
+            interleave(gb, g4)
+            return gb
+
+        def products(c, gb):
+            nc.vector.quantize_mx(out=g_codes[:, c * CH : (c + 1) * CH].bitcast(FP8X4), scales=g_sc[c][:], in_=gb[:])
+            for b in range(K // P):
+                acc = psum.tile([P, CH], F32, name="acc")
+                for h in range(CH // C):
+                    e = c * (CH // C) + h
+                    w, ws = weights(e, b)
+                    nc.tensor.matmul_mx(
+                        out=acc[:, h * C : (h + 1) * C],
+                        lhsT=w,
+                        lhsT_scale=ws,
+                        rhs=g_codes[:, e * C : (e + 1) * C].bitcast(FP8X4),
+                        rhs_scale=g_sc[c][:, h * C : (h + 1) * C],
+                        start=True,
+                        stop=True,
+                    )
+                nc.scalar.copy(dx[b][:, c * CH : (c + 1) * CH], acc[:])
+
+        def shared():
+            db = keep.tile([P, T * PACK], BF16, name="db", align_bytes=64)
+            interleave(db, dy_all)
+            d_codes = keep.tile([P, T], U32, name="d_codes", align_bytes=64)
+            d_sc = keep.tile([P, T], U8, name="d_sc", align_bytes=64)
+            nc.vector.quantize_mx(out=d_codes[:].bitcast(FP8X4), scales=d_sc[:], in_=db[:])
+            for b in range(K // P):
+                acc = psum.tile([P, CH], F32, name="acc")
+                w, ws = weights(E, b)
+                nc.tensor.matmul_mx(
+                    out=acc[:], lhsT=w, lhsT_scale=ws, rhs=d_codes[:].bitcast(FP8X4), rhs_scale=d_sc[:], start=True, stop=True
+                )
+                nc.scalar.copy(ds[b][:], acc[:])
+
+        pending = gather(0)
+        for c in range(1, S // CH):
+            nxt = gather(c)
+            products(c - 1, pending)
+            if c == 2:
+                shared()
+            pending = nxt
+        products(S // CH - 1, pending)
+
+        part = list(ds)
+        for r in range(4):
+            for b in range(K // P):
+                acc_sb = keep.tile([P, T], F32, name="sum%d_%d" % (r, b))
+                nc.vector.tensor_tensor(acc_sb[:], dx[b][:].indirect(pos_t[r][:]), part[b][:], ADD)
+                part[b] = acc_sb
+                if r == 3:
+                    nc.sync.dma_start(out[b * P : (b + 1) * P, :], acc_sb[:])

@@ -4,10 +4,14 @@ import concourse.mybir as mybir
 
 K, T, E, C, N = 384, 512, 8, 256, 512
 S = E * C
+TOP = 4
 P = 128
 PACK = 4
-CH = 512
-WIN = 704
+BANK = 512
+BLOCKS = K // P
+CHUNKS = (768, 512, 512, 256)
+WINDOW = 800
+KIB = 1024
 FLOPS = 2 * K * N * (S + T)
 
 F32 = mybir.dt.float32
@@ -21,119 +25,180 @@ FP4X4 = mybir.dt.float4_e2m1fn_x4
 MULT = mybir.AluOpType.mult
 ADD = mybir.AluOpType.add
 
+GATHERED_AT = (14, 6, 14, 6)
+ROUNDED_AT = (0, 30, 26, 14)
+CODES_AT = (26, 34, 36, 38)
+DY_CAST_AT, DY_CODES_AT, DS0_AT = 4, 16, 14
+
 
 def tile_moe_bds_lin_none_kernel(tc, dyT, w_words, w_scales, gate, offs, pos1, pos2, pos3, pos4, out):
     nc = tc.nc
+    starts = [sum(CHUNKS[:c]) for c in range(len(CHUNKS) + 1)]
     with ExitStack() as ctx:
         keep = ctx.enter_context(tc.tile_pool(name="keep", bufs=1))
-        ring = ctx.enter_context(tc.tile_pool(name="ring", bufs=2))
-        psum = ctx.enter_context(tc.psum_pool(name="psum", bufs=4))
+        arena = ctx.enter_context(tc.tile_pool(name="arena", bufs=1))
+        psum = ctx.enter_context(tc.psum_pool(name="psum", bufs=1))
 
         offs_t = keep.tile([P, S // 16], U16, name="offs_t")
-        nc.sync.dma_start(offs_t[:], offs)
         dy_rows = dyT.rearrange("(p j) t -> p j t", j=PACK)
-        planes = [keep.tile([P, WIN], F32, name="plane%d" % j) for j in range(PACK)]
-        gates = [keep.tile([P, CH], F32, name="gate%d" % c) for c in range(S // CH)]
-        w_sc = keep.tile([P, (E + 1) * K], U8, name="w_sc", align_bytes=64)
-        nc.gpsimd.memset(w_sc[:].bitcast(I32), 0)
+        windows = [keep.tile([P, WINDOW], F32, name="window%d" % j) for j in range(PACK)]
+        gate_t = keep.tile([P, S], F32, name="gate_t")
+        w_scale_t = keep.tile([P, (E + 1) * K], U8, name="w_scale_t", align_bytes=64)
+        w_word_t = keep.tile([P, (E + 1) * 2 * K], U8, name="w_word_t", align_bytes=64)
         for j in range(PACK):
-            nc.gpsimd.memset(planes[j][:, T:WIN], 0.0)
-        nc.sync.dma_start(planes[0][:, 0:T], dy_rows[:, 0, :])
-        nc.sync.dma_start(gates[0][:], gate[0:P, 0:CH])
+            nc.vector.memset(windows[j][:, T:WINDOW], 0.0)
+        nc.vector.memset(w_scale_t[:].bitcast(I32), 0)
+
+        def load_gate(a, z):
+            nc.sync.dma_start(gate_t[:, a:z], gate[0:P, a:z])
+
+        nc.sync.dma_start(windows[0][:, 0:T], dy_rows[:, 0, :])
+        nc.sync.dma_start(offs_t[:], offs)
+        load_gate(0, C)
+        load_gate(C, starts[1])
         for j in range(1, PACK):
-            nc.sync.dma_start(planes[j][:, 0:T], dy_rows[:, j, :])
-        sc_rows = w_scales.rearrange("e a f k -> f (e a) k").bitcast(I32)
-        w_sc_v = w_sc[:].bitcast(I32).rearrange("p (e k) -> p e k", e=E + 1)
-        for q in range(4):
-            nc.sync.dma_start(w_sc_v[32 * q : 32 * q + 4], sc_rows[4 * q : 4 * q + 4])
-        w_t = keep.tile([P, (E + 1) * 2 * K], U8, name="w_t", align_bytes=64)
+            nc.sync.dma_start(windows[j][:, 0:T], dy_rows[:, j, :])
+        load_gate(starts[1], starts[2])
+        load_gate(starts[2], S)
         nc.sync.dma_start(
-            w_t[:].bitcast(I32).rearrange("p (e k) -> p e k", e=E + 1),
+            w_word_t[:].bitcast(I32).rearrange("p (e k) -> p e k", e=E + 1),
             w_words.rearrange("e a p k -> p (e a) k").bitcast(I32),
         )
-        for c in range(1, S // CH):
-            nc.sync.dma_start(gates[c][:], gate[0:P, c * CH : (c + 1) * CH])
-        dy_all = keep.tile([P, PACK, T], F32, name="dy_all")
-        nc.sync.dma_start(dy_all[:], dy_rows)
+        scale_rows = w_scales.rearrange("e a f k -> f (e a) k").bitcast(I32)
+        scale_view = w_scale_t[:].bitcast(I32).rearrange("p (e k) -> p e k", e=E + 1)
+        for q in range(4):
+            nc.sync.dma_start(scale_view[32 * q : 32 * q + 4], scale_rows[4 * q : 4 * q + 4])
         pos_t = []
         for r, pos in enumerate((pos1, pos2, pos3, pos4)):
-            pt = keep.tile([P, T // 16], U16, name="pos%d" % r)
-            nc.sync.dma_start(pt[:], pos)
-            pos_t.append(pt)
+            one_list = keep.tile([P, T // 16], U16, name="pos_t%d" % r)
+            nc.sync.dma_start(one_list[:], pos)
+            pos_t.append(one_list)
 
-        g_codes = keep.tile([P, S], U32, name="g_codes", align_bytes=64)
-        g_sc = [keep.tile([P, CH], U8, name="g_sc%d" % c, align_bytes=64) for c in range(S // CH)]
-        dx = [keep.tile([P, S], F32, name="dx%d" % b) for b in range(K // P)]
-        ds = [keep.tile([P, T], F32, name="ds%d" % b) for b in range(K // P)]
+        g_scales = keep.tile([P, S], U8, name="g_scales", align_bytes=64)
+        dy_scales = keep.tile([P, T], U8, name="dy_scales", align_bytes=64)
+        dy_rounded = keep.tile([P, T * PACK], BF16, name="dy_rounded", align_bytes=64)
+        dx = [keep.tile([P, S], F32, name="dx%d" % b) for b in range(BLOCKS)]
+        gathered, rounded, g_codes, sums = {}, {}, {}, {}
 
-        def weights(e, b):
-            return (
-                w_t[:, e * 2 * K + b * 2 * P : e * 2 * K + (b + 1) * 2 * P].bitcast(FP4X4),
-                w_sc[:, e * K + b * P : e * K + (b + 1) * P],
-            )
+        def placed(shape, dtype, name, kib):
+            return arena.tile(shape, dtype, name=name, offset=kib * KIB, align_bytes=64)
 
         def interleave(dst, src):
             nc.scalar.copy(
-                dst[:].rearrange("p (c i t) -> p c t i", i=4, t=PACK),
-                src[:].rearrange("p t (c i) -> p c t i", i=4),
+                dst.rearrange("p (c i t) -> p c t i", i=4, t=PACK),
+                src.rearrange("p t (c i) -> p c t i", i=4),
             )
 
+        def pieces(c):
+            a, z = starts[c], starts[c + 1]
+            if z == S:
+                return [(a, a + P), (a + P, z)]
+            return [(a, a + BANK), (a + BANK, z)] if z - a > BANK else [(a, z)]
+
         def gather(c):
-            g4 = ring.tile([P, PACK, CH], F32, name="g4")
+            a, z = starts[c], starts[c + 1]
+            gathered[c] = placed([P, PACK, z - a], F32, "gathered%d" % c, GATHERED_AT[c])
             for j in range(PACK):
-                nc.vector.tensor_tensor(
-                    g4[:, j, :], planes[j][:].indirect(offs_t[:, c * CH // 16 : (c + 1) * CH // 16]), gates[c][:], MULT
-                )
-            gb = ring.tile([P, CH * PACK], BF16, name="gb", align_bytes=64)
-            interleave(gb, g4)
-            return gb
-
-        def products(c, gb):
-            nc.vector.quantize_mx(out=g_codes[:, c * CH : (c + 1) * CH].bitcast(FP8X4), scales=g_sc[c][:], in_=gb[:])
-            for b in range(K // P):
-                acc = psum.tile([P, CH], F32, name="acc")
-                for h in range(CH // C):
-                    e = c * (CH // C) + h
-                    w, ws = weights(e, b)
-                    nc.tensor.matmul_mx(
-                        out=acc[:, h * C : (h + 1) * C],
-                        lhsT=w,
-                        lhsT_scale=ws,
-                        rhs=g_codes[:, e * C : (e + 1) * C].bitcast(FP8X4),
-                        rhs_scale=g_sc[c][:, h * C : (h + 1) * C],
-                        start=True,
-                        stop=True,
+                for u, v in ((a, C), (C, z)) if (c, j) == (0, 0) else ((a, z),):
+                    nc.vector.tensor_tensor(
+                        gathered[c][:, j, u - a : v - a],
+                        windows[j][:].indirect(offs_t[:, u // 16 : v // 16]),
+                        gate_t[:, u:v],
+                        MULT,
                     )
-                nc.scalar.copy(dx[b][:, c * CH : (c + 1) * CH], acc[:])
 
-        def shared():
-            db = keep.tile([P, T * PACK], BF16, name="db", align_bytes=64)
-            interleave(db, dy_all)
-            d_codes = keep.tile([P, T], U32, name="d_codes", align_bytes=64)
-            d_sc = keep.tile([P, T], U8, name="d_sc", align_bytes=64)
-            nc.vector.quantize_mx(out=d_codes[:].bitcast(FP8X4), scales=d_sc[:], in_=db[:])
-            for b in range(K // P):
-                acc = psum.tile([P, CH], F32, name="acc")
-                w, ws = weights(E, b)
-                nc.tensor.matmul_mx(
-                    out=acc[:], lhsT=w, lhsT_scale=ws, rhs=d_codes[:].bitcast(FP8X4), rhs_scale=d_sc[:], start=True, stop=True
+        def round_chunk(c):
+            a, z = starts[c], starts[c + 1]
+            rounded[c] = placed([P, (z - a) * PACK], BF16, "rounded%d" % c, ROUNDED_AT[c])
+            for u, v in pieces(c):
+                interleave(rounded[c][:, (u - a) * PACK : (v - a) * PACK], gathered[c][:, :, u - a : v - a])
+
+        def quantise(c):
+            a, z = starts[c], starts[c + 1]
+            g_codes[c] = placed([P, z - a], U32, "g_codes%d" % c, CODES_AT[c])
+            for u, v in pieces(c):
+                nc.vector.quantize_mx(
+                    out=g_codes[c][:, u - a : v - a].bitcast(FP8X4),
+                    scales=g_scales[:, u:v],
+                    in_=rounded[c][:, (u - a) * PACK : (v - a) * PACK],
                 )
-                nc.scalar.copy(ds[b][:], acc[:])
 
-        pending = gather(0)
-        for c in range(1, S // CH):
-            nxt = gather(c)
-            products(c - 1, pending)
-            if c == 2:
-                shared()
-            pending = nxt
-        products(S // CH - 1, pending)
+        def product(acc, e, b, codes, scales):
+            nc.tensor.matmul_mx(
+                out=acc,
+                lhsT=w_word_t[:, 2 * (e * K + b * P) : 2 * (e * K + (b + 1) * P)].bitcast(FP4X4),
+                lhsT_scale=w_scale_t[:, e * K + b * P : e * K + (b + 1) * P],
+                rhs=codes.bitcast(FP8X4),
+                rhs_scale=scales,
+                start=True,
+                stop=True,
+            )
 
-        part = list(ds)
-        for r in range(4):
-            for b in range(K // P):
-                acc_sb = keep.tile([P, T], F32, name="sum%d_%d" % (r, b))
-                nc.vector.tensor_tensor(acc_sb[:], dx[b][:].indirect(pos_t[r][:]), part[b][:], ADD)
-                part[b] = acc_sb
-                if r == 3:
-                    nc.sync.dma_start(out[b * P : (b + 1) * P, :], acc_sb[:])
+        def routed(b, c, a, z, bank, step=C):
+            acc = psum.tile([P, BANK], F32, name="acc", tag="bank%d" % bank)
+            for s in range(a, z, step):
+                product(
+                    acc[:, s - a : s - a + step], s // C, b, g_codes[c][:, s - starts[c] : s - starts[c] + step], g_scales[:, s : s + step]
+                )
+            nc.scalar.copy(dx[b][:, a:z], acc[:, 0 : z - a])
+
+        def routed_chunk(b, c, bank):
+            routed(b, c, starts[c], starts[c + 1], bank)
+
+        def shared(b, bank, dy_codes):
+            acc = psum.tile([P, BANK], F32, name="acc", tag="bank%d" % bank)
+            product(acc[:], E, b, dy_codes[:], dy_scales[:])
+            if b == 0:
+                sums[b] = placed([P, T], F32, "ds0", DS0_AT)
+                nc.vector.tensor_copy(sums[b][:], acc[:])
+            else:
+                sums[b] = keep.tile([P, T], F32, name="ds%d" % b)
+                nc.scalar.copy(sums[b][:], acc[:])
+
+        dy_cast = placed([P, PACK, T], BF16, "dy_cast", DY_CAST_AT)
+        for j in range(PACK):
+            nc.scalar.copy(dy_cast[:, j, :], windows[j][:, 0:T])
+        interleave(dy_rounded[:], dy_cast[:])
+        gather(0)
+        round_chunk(0)
+        gather(1)
+        quantise(0)
+        round_chunk(1)
+        for b in range(BLOCKS):
+            for i, (u, v) in enumerate(pieces(0)):
+                routed(b, 0, u, v, 2 * b + i)
+        gather(2)
+        round_chunk(2)
+        quantise(1)
+        routed_chunk(0, 1, 6)
+        gather(3)
+        round_chunk(3)
+        quantise(2)
+        dy_codes = placed([P, T], U32, "dy_codes", DY_CODES_AT)
+        nc.vector.quantize_mx(out=dy_codes[:].bitcast(FP8X4), scales=dy_scales[:], in_=dy_rounded[:])
+        routed_chunk(0, 2, 0)
+        quantise(3)
+        shared(0, 7, dy_codes)
+        routed(0, 3, starts[3], S, 1, step=P)
+        routed_chunk(1, 3, 2)
+        shared(1, 0, dy_codes)
+        routed_chunk(1, 1, 7)
+        shared(2, 1, dy_codes)
+        routed_chunk(2, 1, 2)
+        routed_chunk(2, 2, 0)
+        routed_chunk(1, 2, 7)
+        routed_chunk(2, 3, 1)
+
+        def combine(b, r, cuts):
+            new_sum = keep.tile([P, T], F32, name="sum%d_%d" % (b, r))
+            for a, z in zip(cuts, cuts[1:]):
+                nc.vector.tensor_tensor(new_sum[:, a:z], dx[b][:].indirect(pos_t[r][:, a // 16 : z // 16]), sums[b][:, a:z], ADD)
+                if r == TOP - 1:
+                    nc.sync.dma_start(out[b * P : (b + 1) * P, a:z], new_sum[:, a:z])
+            sums[b] = new_sum
+
+        for r in range(TOP):
+            combine(0, r, (0, T // 2, T))
+        for r in range(TOP):
+            combine(1, r, (0, T))
+            combine(2, r, (0, T - P, T) if r == TOP - 1 else (0, T))

from contextlib import ExitStack

import concourse.mybir as mybir

K, T, E, C, N = 384, 512, 8, 256, 512
S = E * C
TOP = 4
P = 128
PACK = 4
BANK = 512
BLOCKS = K // P
CHUNKS = (768, 512, 512, 256)
WINDOW = 800
KIB = 1024
FLOPS = 2 * K * N * (S + T)

F32 = mybir.dt.float32
BF16 = mybir.dt.bfloat16
U32 = mybir.dt.uint32
U16 = mybir.dt.uint16
U8 = mybir.dt.uint8
I32 = mybir.dt.int32
FP8X4 = mybir.dt.float8_e4m3fn_x4
FP4X4 = mybir.dt.float4_e2m1fn_x4
MULT = mybir.AluOpType.mult
ADD = mybir.AluOpType.add

GATHERED_AT = (14, 6, 14, 6)
ROUNDED_AT = (0, 30, 26, 14)
CODES_AT = (26, 34, 36, 38)
DY_CAST_AT, DY_CODES_AT, DS0_AT = 4, 16, 14


def tile_moe_bds_lin_none_kernel(tc, dyT, w_words, w_scales, gate, offs, pos1, pos2, pos3, pos4, out):
    nc = tc.nc
    starts = [sum(CHUNKS[:c]) for c in range(len(CHUNKS) + 1)]
    with ExitStack() as ctx:
        keep = ctx.enter_context(tc.tile_pool(name="keep", bufs=1))
        arena = ctx.enter_context(tc.tile_pool(name="arena", bufs=1))
        psum = ctx.enter_context(tc.psum_pool(name="psum", bufs=1))

        offs_t = keep.tile([P, S // 16], U16, name="offs_t")
        dy_rows = dyT.rearrange("(p j) t -> p j t", j=PACK)
        windows = [keep.tile([P, WINDOW], F32, name="window%d" % j) for j in range(PACK)]
        gate_t = keep.tile([P, S], F32, name="gate_t")
        w_scale_t = keep.tile([P, (E + 1) * K], U8, name="w_scale_t", align_bytes=64)
        w_word_t = keep.tile([P, (E + 1) * 2 * K], U8, name="w_word_t", align_bytes=64)
        for j in range(PACK):
            nc.vector.memset(windows[j][:, T:WINDOW], 0.0)
        nc.vector.memset(w_scale_t[:].bitcast(I32), 0)

        def load_gate(a, z):
            nc.sync.dma_start(gate_t[:, a:z], gate[0:P, a:z])

        nc.sync.dma_start(windows[0][:, 0:T], dy_rows[:, 0, :])
        nc.sync.dma_start(offs_t[:], offs)
        load_gate(0, C)
        load_gate(C, starts[1])
        for j in range(1, PACK):
            nc.sync.dma_start(windows[j][:, 0:T], dy_rows[:, j, :])
        load_gate(starts[1], starts[2])
        load_gate(starts[2], S)
        nc.sync.dma_start(
            w_word_t[:].bitcast(I32).rearrange("p (e k) -> p e k", e=E + 1),
            w_words.rearrange("e a p k -> p (e a) k").bitcast(I32),
        )
        scale_rows = w_scales.rearrange("e a f k -> f (e a) k").bitcast(I32)
        scale_view = w_scale_t[:].bitcast(I32).rearrange("p (e k) -> p e k", e=E + 1)
        for q in range(4):
            nc.sync.dma_start(scale_view[32 * q : 32 * q + 4], scale_rows[4 * q : 4 * q + 4])
        pos_t = []
        for r, pos in enumerate((pos1, pos2, pos3, pos4)):
            one_list = keep.tile([P, T // 16], U16, name="pos_t%d" % r)
            nc.sync.dma_start(one_list[:], pos)
            pos_t.append(one_list)

        g_scales = keep.tile([P, S], U8, name="g_scales", align_bytes=64)
        dy_scales = keep.tile([P, T], U8, name="dy_scales", align_bytes=64)
        dy_rounded = keep.tile([P, T * PACK], BF16, name="dy_rounded", align_bytes=64)
        dx = [keep.tile([P, S], F32, name="dx%d" % b) for b in range(BLOCKS)]
        gathered, rounded, g_codes, sums = {}, {}, {}, {}

        def placed(shape, dtype, name, kib):
            return arena.tile(shape, dtype, name=name, offset=kib * KIB, align_bytes=64)

        def interleave(dst, src):
            nc.scalar.copy(
                dst.rearrange("p (c i t) -> p c t i", i=4, t=PACK),
                src.rearrange("p t (c i) -> p c t i", i=4),
            )

        def pieces(c):
            a, z = starts[c], starts[c + 1]
            if z == S:
                return [(a, a + P), (a + P, z)]
            return [(a, a + BANK), (a + BANK, z)] if z - a > BANK else [(a, z)]

        def gather(c):
            a, z = starts[c], starts[c + 1]
            gathered[c] = placed([P, PACK, z - a], F32, "gathered%d" % c, GATHERED_AT[c])
            for j in range(PACK):
                for u, v in ((a, C), (C, z)) if (c, j) == (0, 0) else ((a, z),):
                    nc.vector.tensor_tensor(
                        gathered[c][:, j, u - a : v - a],
                        windows[j][:].indirect(offs_t[:, u // 16 : v // 16]),
                        gate_t[:, u:v],
                        MULT,
                    )

        def round_chunk(c):
            a, z = starts[c], starts[c + 1]
            rounded[c] = placed([P, (z - a) * PACK], BF16, "rounded%d" % c, ROUNDED_AT[c])
            for u, v in pieces(c):
                interleave(rounded[c][:, (u - a) * PACK : (v - a) * PACK], gathered[c][:, :, u - a : v - a])

        def quantise(c):
            a, z = starts[c], starts[c + 1]
            g_codes[c] = placed([P, z - a], U32, "g_codes%d" % c, CODES_AT[c])
            for u, v in pieces(c):
                nc.vector.quantize_mx(
                    out=g_codes[c][:, u - a : v - a].bitcast(FP8X4),
                    scales=g_scales[:, u:v],
                    in_=rounded[c][:, (u - a) * PACK : (v - a) * PACK],
                )

        def product(acc, e, b, codes, scales):
            nc.tensor.matmul_mx(
                out=acc,
                lhsT=w_word_t[:, 2 * (e * K + b * P) : 2 * (e * K + (b + 1) * P)].bitcast(FP4X4),
                lhsT_scale=w_scale_t[:, e * K + b * P : e * K + (b + 1) * P],
                rhs=codes.bitcast(FP8X4),
                rhs_scale=scales,
                start=True,
                stop=True,
            )

        def routed(b, c, a, z, bank, step=C):
            acc = psum.tile([P, BANK], F32, name="acc", tag="bank%d" % bank)
            for s in range(a, z, step):
                product(
                    acc[:, s - a : s - a + step], s // C, b, g_codes[c][:, s - starts[c] : s - starts[c] + step], g_scales[:, s : s + step]
                )
            nc.scalar.copy(dx[b][:, a:z], acc[:, 0 : z - a])

        def routed_chunk(b, c, bank):
            routed(b, c, starts[c], starts[c + 1], bank)

        def shared(b, bank, dy_codes):
            acc = psum.tile([P, BANK], F32, name="acc", tag="bank%d" % bank)
            product(acc[:], E, b, dy_codes[:], dy_scales[:])
            if b == 0:
                sums[b] = placed([P, T], F32, "ds0", DS0_AT)
                nc.vector.tensor_copy(sums[b][:], acc[:])
            else:
                sums[b] = keep.tile([P, T], F32, name="ds%d" % b)
                nc.scalar.copy(sums[b][:], acc[:])

        dy_cast = placed([P, PACK, T], BF16, "dy_cast", DY_CAST_AT)
        for j in range(PACK):
            nc.scalar.copy(dy_cast[:, j, :], windows[j][:, 0:T])
        interleave(dy_rounded[:], dy_cast[:])
        gather(0)
        round_chunk(0)
        gather(1)
        quantise(0)
        round_chunk(1)
        for b in range(BLOCKS):
            for i, (u, v) in enumerate(pieces(0)):
                routed(b, 0, u, v, 2 * b + i)
        gather(2)
        round_chunk(2)
        quantise(1)
        routed_chunk(0, 1, 6)
        gather(3)
        round_chunk(3)
        quantise(2)
        dy_codes = placed([P, T], U32, "dy_codes", DY_CODES_AT)
        nc.vector.quantize_mx(out=dy_codes[:].bitcast(FP8X4), scales=dy_scales[:], in_=dy_rounded[:])
        routed_chunk(0, 2, 0)
        quantise(3)
        shared(0, 7, dy_codes)
        routed(0, 3, starts[3], S, 1, step=P)
        routed_chunk(1, 3, 2)
        shared(1, 0, dy_codes)
        routed_chunk(1, 1, 7)
        shared(2, 1, dy_codes)
        routed_chunk(2, 1, 2)
        routed_chunk(2, 2, 0)
        routed_chunk(1, 2, 7)
        routed_chunk(2, 3, 1)

        def combine(b, r, cuts):
            new_sum = keep.tile([P, T], F32, name="sum%d_%d" % (b, r))
            for a, z in zip(cuts, cuts[1:]):
                nc.vector.tensor_tensor(new_sum[:, a:z], dx[b][:].indirect(pos_t[r][:, a // 16 : z // 16]), sums[b][:, a:z], ADD)
                if r == TOP - 1:
                    nc.sync.dma_start(out[b * P : (b + 1) * P, a:z], new_sum[:, a:z])
            sums[b] = new_sum

        for r in range(TOP):
            combine(0, r, (0, T // 2, T))
        for r in range(TOP):
            combine(1, r, (0, T))
            combine(2, r, (0, T - P, T) if r == TOP - 1 else (0, T))
